import numpy as np
import ml_dtypes


def mxq(x, axis, fmt="e4m3"):
    dtype, down = {"e4m3": (ml_dtypes.float8_e4m3fn, 7), "e5m2": (ml_dtypes.float8_e5m2, 14)}[fmt]
    v = np.moveaxis(np.asarray(x, np.float32).astype(ml_dtypes.bfloat16).astype(np.float64), axis, -1)
    blocks = v.reshape(v.shape[:-1] + (-1, 32))
    amax = np.abs(blocks).max(-1, keepdims=True)
    byte = np.maximum(np.where(amax > 0, np.frexp(amax)[1] - 1 + 127, 0) - down, 1)
    scale = np.exp2(byte - 127.0)
    codes = (blocks / scale).astype(np.float32).astype(dtype).astype(np.float64)
    return np.moveaxis((codes * scale).reshape(v.shape), -1, axis)


WIDE = False


def mx_kscale(k):
    if not WIDE:
        return np.ones(k)
    levels = np.array([10, -10, 5, -5, 0])
    if k % 512:
        return np.exp2(np.random.permutation(np.resize(levels, k // 32))).repeat(32)
    a = np.empty((k // 512, 16))
    for p in range(k // 512):
        a[p, :8] = np.random.permutation(np.resize(levels, 8))
        for g in range(8):
            far = levels[np.abs(levels - a[p, g]) >= 10]
            a[p, g + 8] = far[np.random.randint(len(far))]
    return np.exp2(a.ravel()).repeat(32)


def f64(x):
    return np.asarray(x).astype(np.float64)


def striped(idx):
    return np.tile(idx.reshape(-1, 16).T, (8, 1)).astype(np.uint16)


def unstriped(offs):
    return offs[:16].T.reshape(-1).astype(np.int64)


def striped8(idx):
    return np.concatenate([x.reshape(-1, 16).T for x in idx]).astype(np.uint16)


def runs(offs, k):
    lists = np.stack([offs[16 * r : 16 * r + 16].T.reshape(-1) for r in range(8)]).astype(np.int64)
    return lists[np.arange(k) % 512 // 64]


def pack_weight(w):
    k, n = w.shape
    w = f64(np.asarray(w, np.float32).astype(ml_dtypes.bfloat16)).reshape(k // 32, 32, n)
    amax = np.abs(w).max(1)
    byte = np.clip(np.where(amax > 0, np.frexp(amax)[1] - 1 + 127 - 7, 1), 1, 254)
    scaled = (w * np.exp2(127.0 - byte)[:, None, :]).reshape(k, n).astype(np.float32)
    words = np.ascontiguousarray(scaled.reshape(k // 512, 128, 4, n).transpose(0, 1, 3, 2)).astype(ml_dtypes.float8_e4m3fn).view(np.uint8)
    return words, np.ascontiguousarray(byte.astype(np.uint8).reshape(k // 512, 16, n))


def unpack_weight(words, scales):
    g, p, n, _ = words.shape
    vals = np.ascontiguousarray(words).view(ml_dtypes.float8_e4m3fn).astype(np.float64) * np.repeat(np.exp2(scales.astype(np.float64) - 127.0), 8, axis=1)[..., None]
    return vals.transpose(0, 1, 3, 2).reshape(g * 512, n)


K, T, S, N, H, W = 512, 2048, 512, 512, 512, 256


def setup_inputs():
    n = np.random.standard_normal
    s = mx_kscale(K)[:, None]
    u = mx_kscale(H)
    packed_xT = pack_weight(n((K, T)) * s)
    perm = np.stack([np.random.permutation(S) for _ in range(8)])
    return {
        "x_words": packed_xT[0],
        "x_scales": packed_xT[1],
        "w1": (n((K, H)) / np.sqrt(K) / s).astype(np.float32),
        "gn": (np.random.uniform(0.5, 1.5, (H, 1)) * u[:, None]).astype(np.float32),
        "w2": (n((H, N)) / np.sqrt(H) / u[:, None]).astype(np.float32),
        "offs": striped(np.random.permutation(T)[:S]),
        "n1": striped8(perm[:, :W]),
        "n2": striped8(perm[:, W:]),
        "n3": striped8(np.stack([np.random.permutation(S) for _ in range(8)])),
        "n4": striped8(np.stack([np.random.permutation(S) for _ in range(8)])),
        "n5": striped8(np.stack([np.random.permutation(S) for _ in range(8)])),
        "n6": striped8(np.stack([np.random.permutation(S) for _ in range(8)])),
    }


def reference(x_words, x_scales, w1, gn, w2, offs, n1, n2, n3, n4, n5, n6):
    xq = unpack_weight(x_words, x_scales)[:, unstriped(offs)]
    y = mxq(f64(w1), 0, "e4m3").T @ xq
    pb = y[np.arange(H)[:, None], runs(n2, H)]
    pa = y[np.arange(H)[:, None], runs(n1, H)]
    rb = pb - (0.5 * pa)
    ra = np.sqrt((pa) ** 2 + (pb) ** 2 + 0.25)
    ds = np.zeros((H, S))
    ds[np.arange(H)[:, None], runs(n1, H)] = ra
    dt = ds.copy()
    dt[np.arange(H)[:, None], runs(n2, H)] = rb
    z = f64(gn) * dt
    h = mxq(f64(w2), 0, "e4m3").T @ mxq(z, 0, "e4m3")
    return np.maximum(h[np.arange(N)[:, None], runs(n3, N)] + y[np.arange(H)[:, None], runs(n5, H)], h[np.arange(N)[:, None], runs(n4, N)] + y[np.arange(H)[:, None], runs(n6, H)])

@@ -1,0 +1,207 @@
+from contextlib import ExitStack
+
+import concourse.mybir as mybir
+
+K, T, S, H, W = 512, 2048, 512, 512, 256
+FLOPS = 2 * K * H * S + 2 * H * H * S
+
+F32 = mybir.dt.float32
+BF16 = mybir.dt.bfloat16
+I32 = mybir.dt.int32
+U32 = mybir.dt.uint32
+U16 = mybir.dt.uint16
+U8 = mybir.dt.uint8
+FP8X4 = mybir.dt.float8_e4m3fn_x4
+ACT = mybir.ActivationFunctionType
+ALU = mybir.AluOpType
+
+P = 128
+PACK = 4
+HALF = 256
+LIST_HALF = HALF // 16
+
+
+def tile_picked_skippathbpolar_none_p_kernel(
+    tc, x_words, x_scales, w1, gn, w2, offs, n1, n2, n3, n4, n5, n6, out
+):
+    nc = tc.nc
+    with ExitStack() as ctx:
+        sb = ctx.enter_context(tc.tile_pool(name="sb", bufs=1))
+        ps = ctx.enter_context(tc.psum_pool(name="ps", bufs=1))
+
+        def load_list(src, name):
+            tl = sb.tile(list(src.shape), U16, name=name)
+            nc.sync.dma_start(tl[:], src)
+            return tl
+
+        def load_weight(src, name):
+            rows = src.rearrange("(p j) c -> p j c", j=PACK)
+            halves = []
+            for u in range(2):
+                raw = sb.tile([P, PACK, HALF], F32, name="%s_raw%d" % (name, u))
+                nc.sync.dma_start(raw[:], rows[:, :, u * HALF : (u + 1) * HALF])
+                halves.append(raw)
+            return halves
+
+        def quantize_weight(halves, name, width, first_on_scalar):
+            grouped = sb.tile([P, PACK, P, PACK], BF16, name=name + "_bf", align_bytes=64)
+            codes = sb.tile([P, H], U32, name=name + "_codes", align_bytes=64)
+            scales = sb.tile([P, H], U8, name=name + "_scales", align_bytes=64)
+            for u in range(2):
+                dst = grouped[:, :, 64 * u : 64 * (u + 1), :].rearrange("p t m j -> p m t j")
+                src = halves[u][:].rearrange("p j (m t) -> p m t j", t=PACK)
+                if u == 0 and first_on_scalar:
+                    nc.scalar.activation(dst, src, ACT.Copy)
+                else:
+                    nc.vector.tensor_copy(out=dst, in_=src)
+            flat = grouped[:].rearrange("p t m j -> p (t m j)")
+            for c in range(0, H, width):
+                nc.vector.quantize_mx(
+                    out=codes[:, c : c + width].bitcast(FP8X4),
+                    scales=scales[:, c : c + width],
+                    in_=flat[:, PACK * c : PACK * (c + width)],
+                )
+            return codes, scales
+
+        xs_all = sb.tile([P, T], U8, name="xs_all", tag="x_slot", align_bytes=64)
+        nc.vector.memset(xs_all[:].bitcast(I32), 0)
+        for q in range(4):
+            nc.scalar.dma_start(
+                xs_all[32 * q : 32 * q + 4, :].bitcast(I32), x_scales[0, 4 * q : 4 * q + 4, :].bitcast(I32)
+            )
+        offs_t = load_list(offs, "offs_t")
+        n1_t = load_list(n1, "n1_t")
+        n2_t = load_list(n2, "n2_t")
+        n5_t = load_list(n5, "n5_t")
+        w1_raw = load_weight(w1, "w1")
+        xw_all = sb.tile([P, T], U32, name="xw_all")
+        nc.sync.dma_start(xw_all[:].bitcast(I32), x_words[0].rearrange("p n t -> p (n t)").bitcast(I32))
+        w2_raw = load_weight(w2, "w2")
+        gain = sb.tile([P, PACK], F32, name="gain")
+        nc.sync.dma_start(gain[:], gn.rearrange("(p t) o -> p (t o)", t=PACK))
+        n6_t = load_list(n6, "n6_t")
+        n3_t = load_list(n3, "n3_t")
+        n4_t = load_list(n4, "n4_t")
+
+        quarter = sb.tile([P, 1], F32, name="quarter")
+        nc.vector.memset(quarter[:], 0.25)
+
+        xs = sb.tile([P, S], U8, name="xs", align_bytes=64)
+        nc.vector.tensor_copy(xs[:], xs_all[:].indirect(offs_t[:]))
+        w1_codes, w1_scales = quantize_weight(w1_raw, "w1", H, True)
+        xw = sb.tile([P, S], U32, name="xw", tag="x_slot", align_bytes=64)
+        nc.vector.tensor_copy(xw[:], xw_all[:].indirect(offs_t[:]))
+
+        def product(codes, scales, rhs, rhs_scales, t, name):
+            acc = ps.tile([P, S], F32, name="%s_ps%d" % (name, t))
+            cols = slice(P * t, P * (t + 1))
+            nc.tensor.matmul_mx(
+                out=acc[:],
+                lhsT=codes[:, cols].bitcast(FP8X4),
+                lhsT_scale=scales[:, cols],
+                rhs=rhs[:].bitcast(FP8X4),
+                rhs_scale=rhs_scales[:],
+                start=True,
+                stop=True,
+            )
+            res = sb.tile([P, S], F32, name="%s%d" % (name, t))
+            nc.scalar.copy(res[:], acc[:])
+            return res
+
+        w2_codes, w2_scales = quantize_weight(w2_raw, "w2", H, False)
+
+        def halves_of(lst):
+            return [(slice(HALF * u, HALF * (u + 1)), lst[:, LIST_HALF * u : LIST_HALF * (u + 1)]) for u in range(2)]
+
+        def fetch(window, lst, name, **slot):
+            res = sb.tile([P, S], F32, name=name, **slot)
+            for cols, part in halves_of(lst):
+                nc.scalar.activation(res[:, cols], window[:].indirect(part), ACT.Copy)
+            return res
+
+        planes = sb.tile([P, PACK - 1, S], BF16, name="planes")
+        y, ssum, dt = [], [], []
+
+        def pair_up(t):
+            y.append(product(w1_codes, w1_scales, xw, xs, t, "y"))
+            pair = sb.tile([P, 2, W], F32, name="pair%d" % t)
+            nc.scalar.activation(pair[:, 0, :], y[t][:].indirect(n1_t[:]), ACT.Copy, scale=-0.5)
+            if t < 2:
+                nc.vector.tensor_copy(pair[:, 1, :], y[t][:].indirect(n2_t[:]))
+            else:
+                nc.scalar.activation(pair[:, 1, :], y[t][:].indirect(n2_t[:]), ACT.Copy)
+            if t == 1:
+                root(0)
+            sq = sb.tile([P, 2, W], F32, name="sq%d" % t)
+            nc.scalar.activation(sq[:], pair[:], ACT.Square)
+            dt.append(sb.tile([P, S], F32, name="dt%d" % t))
+            nc.vector.tensor_tensor(dt[t][:].indirect(n2_t[:]), pair[:, 1, :], pair[:, 0, :], ALU.add)
+            ssum.append(sb.tile([P, W], F32, name="ssum%d" % t))
+            nc.vector.scalar_tensor_tensor(ssum[t][:], sq[:, 0, :], 4.0, sq[:, 1, :], ALU.mult, ALU.add)
+
+        def root(t):
+            ra = sb.tile([P, W], F32, name="ra%d" % t)
+            nc.scalar.activation(ra[:], ssum[t][:], ACT.Sqrt, bias=quarter[:])
+            nc.vector.tensor_copy(dt[t][:].indirect(n1_t[:]), ra[:])
+
+        def scale_plane(t):
+            nc.scalar.activation(planes[:, t, :], dt[t][:], ACT.Copy, scale=gain[:, t : t + 1])
+
+        y5, y6 = [], []
+        pair_up(0)
+        pair_up(1)
+        pair_up(2)
+        root(1)
+        pair_up(3)
+        scale_plane(0)
+        root(2)
+        y5.append(fetch(y[0], n5_t, "y5_0", tag="y5_slot"))
+        scale_plane(1)
+        root(3)
+        y6.append(fetch(y[0], n6_t, "y6_0"))
+        scale_plane(2)
+        y5.append(fetch(y[1], n5_t, "y5_1"))
+        y6.append(fetch(y[1], n6_t, "y6_1"))
+        y5.append(fetch(y[2], n5_t, "y5_2"))
+        y6.append(fetch(y[2], n6_t, "y6_2"))
+
+        z_bf = sb.tile([P, S, PACK], BF16, name="z_bf", tag="z_slot", align_bytes=64)
+        z_codes = sb.tile([P, S], U32, name="z_codes", align_bytes=64)
+        z_scales = sb.tile([P, S], U8, name="z_scales", align_bytes=64)
+        nc.vector.tensor_copy(z_bf[:, :, 0 : PACK - 1], planes[:].rearrange("p t c -> p c t"))
+        last = PACK - 1
+        nc.vector.tensor_scalar(z_bf[:, :, last], dt[last][:], gain[:, last : last + 1], None, ALU.mult)
+        nc.vector.quantize_mx(
+            out=z_codes[:].bitcast(FP8X4), scales=z_scales[:], in_=z_bf[:].rearrange("p c t -> p (c t)")
+        )
+        y5_last = sb.tile([P, S], F32, name="y5_last", tag="z_slot", align_bytes=64)
+        for cols, part in halves_of(n5_t):
+            nc.vector.tensor_copy(y5_last[:, cols], y[last][:].indirect(part))
+        y5.append(y5_last)
+
+        out_rows = out.rearrange("(p t) c -> p t c", t=PACK)
+        h, first = [], []
+
+        def start(t):
+            h.append(product(w2_codes, w2_scales, z_codes, z_scales, t, "h"))
+            first.append(sb.tile([P, S], F32, name="first%d" % t))
+            for cols, part in halves_of(n3_t):
+                nc.vector.tensor_tensor(first[t][:, cols], h[t][:].indirect(part), y5[t][:, cols], ALU.add)
+
+        def end(t):
+            h4 = fetch(h[t], n4_t, "h4_%d" % t)
+            second = sb.tile([P, S], F32, name="second%d" % t)
+            nc.vector.tensor_tensor(second[:], h4[:], y6[t][:], ALU.add)
+            res = sb.tile([P, S], F32, name="res%d" % t)
+            nc.vector.tensor_tensor(res[:], first[t][:], second[:], ALU.max)
+            nc.sync.dma_start(out_rows[:, t, :], res[:])
+
+        start(0)
+        start(1)
+        end(0)
+        start(2)
+        end(1)
+        start(3)
+        end(2)
+        y6.append(fetch(y[last], n6_t, "y6_3", tag="y5_slot"))
+        end(3)

@@ -34,51 +34,50 @@ def tile_picked_skippathbpolar_none_p_kernel(
             nc.sync.dma_start(tl[:], src)
             return tl
 
-        def load_weight(src, name):
+        def load_half(src, name, u):
             rows = src.rearrange("(p j) c -> p j c", j=PACK)
-            halves = []
-            for u in range(2):
-                raw = sb.tile([P, PACK, HALF], F32, name="%s_raw%d" % (name, u))
-                nc.sync.dma_start(raw[:], rows[:, :, u * HALF : (u + 1) * HALF])
-                halves.append(raw)
-            return halves
+            raw = sb.tile([P, PACK, HALF], F32, name="%s_raw%d" % (name, u))
+            nc.sync.dma_start(raw[:], rows[:, :, u * HALF : (u + 1) * HALF])
+            return raw
 
-        def quantize_weight(halves, name, width, first_on_scalar):
+        def group_weight(grouped, halves, lo, hi, engine):
+            u, c0 = divmod(lo, HALF)
+            dst = grouped[:, :, lo // PACK : hi // PACK, :].rearrange("p t m j -> p m t j")
+            src = halves[u][:, :, c0 : c0 + hi - lo].rearrange("p j (m t) -> p m t j", t=PACK)
+            if engine == "scalar":
+                nc.scalar.activation(dst, src, ACT.Copy)
+            else:
+                nc.vector.tensor_copy(out=dst, in_=src)
+
+        def quantize_weight(halves, name, shares, cuts):
             grouped = sb.tile([P, PACK, P, PACK], BF16, name=name + "_bf", align_bytes=64)
             codes = sb.tile([P, H], U32, name=name + "_codes", align_bytes=64)
             scales = sb.tile([P, H], U8, name=name + "_scales", align_bytes=64)
-            for u in range(2):
-                dst = grouped[:, :, 64 * u : 64 * (u + 1), :].rearrange("p t m j -> p m t j")
-                src = halves[u][:].rearrange("p j (m t) -> p m t j", t=PACK)
-                if u == 0 and first_on_scalar:
-                    nc.scalar.activation(dst, src, ACT.Copy)
-                else:
-                    nc.vector.tensor_copy(out=dst, in_=src)
+            for lo, hi, engine in shares:
+                group_weight(grouped, halves, lo, hi, engine)
             flat = grouped[:].rearrange("p t m j -> p (t m j)")
-            for c in range(0, H, width):
+            for lo, hi in cuts:
                 nc.vector.quantize_mx(
-                    out=codes[:, c : c + width].bitcast(FP8X4),
-                    scales=scales[:, c : c + width],
-                    in_=flat[:, PACK * c : PACK * (c + width)],
+                    out=codes[:, lo:hi].bitcast(FP8X4), scales=scales[:, lo:hi], in_=flat[:, PACK * lo : PACK * hi]
                 )
             return codes, scales
 
-        xs_all = sb.tile([P, T], U8, name="xs_all", tag="x_slot", align_bytes=64)
+        xs_all = sb.tile([P, T], U8, name="xs_all")
         nc.vector.memset(xs_all[:].bitcast(I32), 0)
-        for q in range(4):
-            nc.scalar.dma_start(
-                xs_all[32 * q : 32 * q + 4, :].bitcast(I32), x_scales[0, 4 * q : 4 * q + 4, :].bitcast(I32)
-            )
+        for r in range(4):
+            nc.sync.dma_start(xs_all[r:P:32, :].bitcast(I32), x_scales[0, r:16:4, :].bitcast(I32))
         offs_t = load_list(offs, "offs_t")
-        n1_t = load_list(n1, "n1_t")
-        n2_t = load_list(n2, "n2_t")
-        n5_t = load_list(n5, "n5_t")
-        w1_raw = load_weight(w1, "w1")
         xw_all = sb.tile([P, T], U32, name="xw_all")
         nc.sync.dma_start(xw_all[:].bitcast(I32), x_words[0].rearrange("p n t -> p (n t)").bitcast(I32))
-        w2_raw = load_weight(w2, "w2")
+        w1_raw = [load_half(w1, "w1", 0)]
+        n1_t = load_list(n1, "n1_t")
+        w1_raw.append(load_half(w1, "w1", 1))
+        w2_raw = [load_half(w2, "w2", 0)]
+        n2_t = load_list(n2, "n2_t")
+        w2_raw.append(load_half(w2, "w2", 1))
         gain = sb.tile([P, PACK], F32, name="gain")
         nc.sync.dma_start(gain[:], gn.rearrange("(p t) o -> p (t o)", t=PACK))
+        n5_t = load_list(n5, "n5_t")
         n6_t = load_list(n6, "n6_t")
         n3_t = load_list(n3, "n3_t")
         n4_t = load_list(n4, "n4_t")
@@ -86,53 +85,57 @@ def tile_picked_skippathbpolar_none_p_kernel(
         quarter = sb.tile([P, 1], F32, name="quarter")
         nc.vector.memset(quarter[:], 0.25)
 
+        xw = sb.tile([P, S], U32, name="xw", align_bytes=64)
+        nc.vector.tensor_copy(xw[:], xw_all[:].indirect(offs_t[:]))
         xs = sb.tile([P, S], U8, name="xs", align_bytes=64)
         nc.vector.tensor_copy(xs[:], xs_all[:].indirect(offs_t[:]))
-        w1_codes, w1_scales = quantize_weight(w1_raw, "w1", H, True)
-        xw = sb.tile([P, S], U32, name="xw", tag="x_slot", align_bytes=64)
-        nc.vector.tensor_copy(xw[:], xw_all[:].indirect(offs_t[:]))
+        w1_codes, w1_scales = quantize_weight(
+            w1_raw, "w1", [(0, 256, "scalar"), (256, 512, "vector")], [(0, P), (P, H)]
+        )
 
-        def product(codes, scales, rhs, rhs_scales, t, name):
+        def product(codes, scales, rhs, rhs_scales, t, name, width):
             acc = ps.tile([P, S], F32, name="%s_ps%d" % (name, t))
             cols = slice(P * t, P * (t + 1))
-            nc.tensor.matmul_mx(
-                out=acc[:],
-                lhsT=codes[:, cols].bitcast(FP8X4),
-                lhsT_scale=scales[:, cols],
-                rhs=rhs[:].bitcast(FP8X4),
-                rhs_scale=rhs_scales[:],
-                start=True,
-                stop=True,
-            )
+            for c in range(0, S, width):
+                nc.tensor.matmul_mx(
+                    out=acc[:, c : c + width],
+                    lhsT=codes[:, cols].bitcast(FP8X4),
+                    lhsT_scale=scales[:, cols],
+                    rhs=rhs[:, c : c + width].bitcast(FP8X4),
+                    rhs_scale=rhs_scales[:, c : c + width],
+                    start=True,
+                    stop=True,
+                )
             res = sb.tile([P, S], F32, name="%s%d" % (name, t))
             nc.scalar.copy(res[:], acc[:])
             return res
 
-        w2_codes, w2_scales = quantize_weight(w2_raw, "w2", H, False)
+        w2_codes, w2_scales = quantize_weight(w2_raw, "w2", [(0, 256, "scalar"), (256, 512, "vector")], [(0, H)])
 
         def halves_of(lst):
             return [(slice(HALF * u, HALF * (u + 1)), lst[:, LIST_HALF * u : LIST_HALF * (u + 1)]) for u in range(2)]
 
-        def fetch(window, lst, name, **slot):
-            res = sb.tile([P, S], F32, name=name, **slot)
+        def fetch(window, lst, name):
+            res = sb.tile([P, S], F32, name=name)
             for cols, part in halves_of(lst):
                 nc.scalar.activation(res[:, cols], window[:].indirect(part), ACT.Copy)
             return res
 
-        planes = sb.tile([P, PACK - 1, S], BF16, name="planes")
+        planes = sb.tile([P, PACK, S], BF16, name="planes")
         y, ssum, dt = [], [], []
 
         def pair_up(t):
-            y.append(product(w1_codes, w1_scales, xw, xs, t, "y"))
-            pair = sb.tile([P, 2, W], F32, name="pair%d" % t)
+            pair = sb.tile([P, 2, W], F32, name="pair%d" % t, tag="pair%d" % t)
             nc.scalar.activation(pair[:, 0, :], y[t][:].indirect(n1_t[:]), ACT.Copy, scale=-0.5)
-            if t < 2:
+            if t == 0:
                 nc.vector.tensor_copy(pair[:, 1, :], y[t][:].indirect(n2_t[:]))
             else:
                 nc.scalar.activation(pair[:, 1, :], y[t][:].indirect(n2_t[:]), ACT.Copy)
-            if t == 1:
-                root(0)
-            sq = sb.tile([P, 2, W], F32, name="sq%d" % t)
+            if t + 1 < PACK:
+                y.append(product(w1_codes, w1_scales, xw, xs, t + 1, "y", S))
+            else:
+                scale_plane(0)
+            sq = sb.tile([P, 2, W], F32, name="sq%d" % t, tag="sq%d" % t)
             nc.scalar.activation(sq[:], pair[:], ACT.Square)
             dt.append(sb.tile([P, S], F32, name="dt%d" % t))
             nc.vector.tensor_tensor(dt[t][:].indirect(n2_t[:]), pair[:, 1, :], pair[:, 0, :], ALU.add)
@@ -147,61 +150,93 @@ def tile_picked_skippathbpolar_none_p_kernel(
         def scale_plane(t):
             nc.scalar.activation(planes[:, t, :], dt[t][:], ACT.Copy, scale=gain[:, t : t + 1])
 
-        y5, y6 = [], []
+        y5, y6 = {}, {}
+        skips = [
+            (dst, slot, t, cols, part)
+            for t in range(PACK)
+            for dst, lst, slot in ((y5, n5_t, "sq"), (y6, n6_t, "pair"))
+            for cols, part in halves_of(lst)
+            if (slot, t) != ("sq", PACK - 1)
+        ]
+
+        def fetch_skips(count):
+            for dst, slot, t, cols, part in skips[:count]:
+                if t not in dst:
+                    dst[t] = sb.tile([P, S], F32, name="skip_%s%d" % (slot, t), tag="%s%d" % (slot, t))
+                nc.scalar.activation(dst[t][:, cols], y[t][:].indirect(part), ACT.Copy)
+            return skips[count:]
+
+        y.append(product(w1_codes, w1_scales, xw, xs, 0, "y", S))
         pair_up(0)
         pair_up(1)
+        root(0)
         pair_up(2)
+        skips = fetch_skips(2)
         root(1)
         pair_up(3)
-        scale_plane(0)
+        skips = fetch_skips(1)
         root(2)
-        y5.append(fetch(y[0], n5_t, "y5_0", tag="y5_slot"))
+        skips = fetch_skips(1)
         scale_plane(1)
+        skips = fetch_skips(1)
         root(3)
-        y6.append(fetch(y[0], n6_t, "y6_0"))
+        skips = fetch_skips(3)
         scale_plane(2)
-        y5.append(fetch(y[1], n5_t, "y5_1"))
-        y6.append(fetch(y[1], n6_t, "y6_1"))
-        y5.append(fetch(y[2], n5_t, "y5_2"))
-        y6.append(fetch(y[2], n6_t, "y6_2"))
+        skips = fetch_skips(6)
 
         z_bf = sb.tile([P, S, PACK], BF16, name="z_bf", tag="z_slot", align_bytes=64)
         z_codes = sb.tile([P, S], U32, name="z_codes", align_bytes=64)
         z_scales = sb.tile([P, S], U8, name="z_scales", align_bytes=64)
-        nc.vector.tensor_copy(z_bf[:, :, 0 : PACK - 1], planes[:].rearrange("p t c -> p c t"))
         last = PACK - 1
-        nc.vector.tensor_scalar(z_bf[:, :, last], dt[last][:], gain[:, last : last + 1], None, ALU.mult)
-        nc.vector.quantize_mx(
-            out=z_codes[:].bitcast(FP8X4), scales=z_scales[:], in_=z_bf[:].rearrange("p c t -> p (c t)")
-        )
+        spans = [slice(0, HALF), slice(HALF, S)]
+        for cols in spans:
+            nc.vector.tensor_scalar(planes[:, last, cols], dt[last][:, cols], gain[:, last : last + 1], None, ALU.mult)
+        for cols in spans:
+            nc.vector.tensor_copy(
+                z_bf[:, cols, :].rearrange("p (c i) t -> p c t i", i=4),
+                planes[:, :, cols].rearrange("p t (c i) -> p c t i", i=4),
+            )
+        for cols in spans:
+            nc.vector.quantize_mx(
+                out=z_codes[:, cols].bitcast(FP8X4),
+                scales=z_scales[:, cols],
+                in_=z_bf[:, cols, :].rearrange("p c t -> p (c t)"),
+            )
         y5_last = sb.tile([P, S], F32, name="y5_last", tag="z_slot", align_bytes=64)
         for cols, part in halves_of(n5_t):
             nc.vector.tensor_copy(y5_last[:, cols], y[last][:].indirect(part))
-        y5.append(y5_last)
+        y5[last] = y5_last
 
         out_rows = out.rearrange("(p t) c -> p t c", t=PACK)
-        h, first = [], []
+        h, first = {}, {}
 
-        def start(t):
-            h.append(product(w2_codes, w2_scales, z_codes, z_scales, t, "h"))
-            first.append(sb.tile([P, S], F32, name="first%d" % t))
-            for cols, part in halves_of(n3_t):
-                nc.vector.tensor_tensor(first[t][:, cols], h[t][:].indirect(part), y5[t][:, cols], ALU.add)
+        def start(t, fused):
+            h[t] = product(w2_codes, w2_scales, z_codes, z_scales, t, "h", HALF if t == 0 else S)
+            first[t] = sb.tile([P, S], F32, name="first%d" % t)
+            if fused:
+                for cols, part in halves_of(n3_t):
+                    nc.vector.tensor_tensor(first[t][:, cols], h[t][:].indirect(part), y5[t][:, cols], ALU.add)
 
-        def end(t):
+        def unfused(t):
+            h3 = fetch(h[t], n3_t, "h3_%d" % t)
+            nc.vector.tensor_tensor(first[t][:], h3[:], y5[t][:], ALU.add)
+
+        def end(t, pieces):
             h4 = fetch(h[t], n4_t, "h4_%d" % t)
             second = sb.tile([P, S], F32, name="second%d" % t)
-            nc.vector.tensor_tensor(second[:], h4[:], y6[t][:], ALU.add)
             res = sb.tile([P, S], F32, name="res%d" % t)
-            nc.vector.tensor_tensor(res[:], first[t][:], second[:], ALU.max)
-            nc.sync.dma_start(out_rows[:, t, :], res[:])
+            for cols in pieces:
+                nc.vector.tensor_tensor(second[:, cols], h4[:, cols], y6[t][:, cols], ALU.add)
+                nc.vector.tensor_tensor(res[:, cols], first[t][:, cols], second[:, cols], ALU.max)
+                nc.sync.dma_start(out_rows[:, t, cols], res[:, cols])
 
-        start(0)
-        start(1)
-        end(0)
-        start(2)
-        end(1)
-        start(3)
-        end(2)
-        y6.append(fetch(y[last], n6_t, "y6_3", tag="y5_slot"))
-        end(3)
+        whole = [slice(0, S)]
+        start(0, True)
+        start(1, True)
+        end(0, whole)
+        start(2, True)
+        end(1, whole)
+        start(3, False)
+        end(2, whole)
+        unfused(3)
+        end(3, spans)

@@ -85,6 +85,9 @@ def tile_picked_skippathbpolar_none_p_kernel(
         quarter = sb.tile([P, 1], F32, name="quarter")
         nc.vector.memset(quarter[:], 0.25)
 
+        warm = sb.tile([P, 1], F32, name="warm")
+        nc.scalar.activation(warm[:], quarter[:], ACT.Sqrt)
+
         xw = sb.tile([P, S], U32, name="xw", align_bytes=64)
         nc.vector.tensor_copy(xw[:], xw_all[:].indirect(offs_t[:]))
         xs = sb.tile([P, S], U8, name="xs", align_bytes=64)

@@ -34,34 +34,21 @@ def tile_picked_skippathbpolar_none_p_kernel(
             nc.sync.dma_start(tl[:], src)
             return tl
 
-        def load_half(src, name, u):
-            rows = src.rearrange("(p j) c -> p j c", j=PACK)
-            raw = sb.tile([P, PACK, HALF], F32, name="%s_raw%d" % (name, u))
-            nc.sync.dma_start(raw[:], rows[:, :, u * HALF : (u + 1) * HALF])
-            return raw
-
-        def group_weight(grouped, halves, lo, hi, engine):
-            u, c0 = divmod(lo, HALF)
-            dst = grouped[:, :, lo // PACK : hi // PACK, :].rearrange("p t m j -> p m t j")
-            src = halves[u][:, :, c0 : c0 + hi - lo].rearrange("p j (m t) -> p m t j", t=PACK)
+        def group(dst, src, engine):
             if engine == "scalar":
                 nc.scalar.activation(dst, src, ACT.Copy)
             else:
                 nc.vector.tensor_copy(out=dst, in_=src)
 
-        def quantize_weight(halves, name, shares, cuts):
-            grouped = sb.tile([P, PACK, P, PACK], BF16, name=name + "_bf", align_bytes=64)
+        def operand(name):
             codes = sb.tile([P, H], U32, name=name + "_codes", align_bytes=64)
             scales = sb.tile([P, H], U8, name=name + "_scales", align_bytes=64)
-            for lo, hi, engine in shares:
-                group_weight(grouped, halves, lo, hi, engine)
-            flat = grouped[:].rearrange("p t m j -> p (t m j)")
-            for lo, hi in cuts:
-                nc.vector.quantize_mx(
-                    out=codes[:, lo:hi].bitcast(FP8X4), scales=scales[:, lo:hi], in_=flat[:, PACK * lo : PACK * hi]
-                )
             return codes, scales
 
+        def quantize(codes, scales, cols, values):
+            nc.vector.quantize_mx(out=codes[:, cols].bitcast(FP8X4), scales=scales[:, cols], in_=values)
+
+        spans = [slice(0, HALF), slice(HALF, S)]
         xs_all = sb.tile([P, T], U8, name="xs_all")
         nc.vector.memset(xs_all[:].bitcast(I32), 0)
         for r in range(4):
@@ -69,12 +56,15 @@ def tile_picked_skippathbpolar_none_p_kernel(
         offs_t = load_list(offs, "offs_t")
         xw_all = sb.tile([P, T], U32, name="xw_all")
         nc.sync.dma_start(xw_all[:].bitcast(I32), x_words[0].rearrange("p n t -> p (n t)").bitcast(I32))
-        w1_raw = [load_half(w1, "w1", 0)]
         n1_t = load_list(n1, "n1_t")
-        w1_raw.append(load_half(w1, "w1", 1))
-        w2_raw = [load_half(w2, "w2", 0)]
         n2_t = load_list(n2, "n2_t")
-        w2_raw.append(load_half(w2, "w2", 1))
+        w1_raw = sb.tile([P, PACK, H], F32, name="w1_raw")
+        nc.sync.dma_start(w1_raw[:], w1.rearrange("(p j) c -> p j c", j=PACK))
+        w2_raw = []
+        for cols in spans:
+            raw = sb.tile([P, PACK, HALF], F32, name="w2_raw%d" % cols.start)
+            nc.sync.dma_start(raw[:], w2.rearrange("(p j) c -> p j c", j=PACK)[:, :, cols])
+            w2_raw.append(raw)
         gain = sb.tile([P, PACK], F32, name="gain")
         nc.sync.dma_start(gain[:], gn.rearrange("(p t) o -> p (t o)", t=PACK))
         n5_t = load_list(n5, "n5_t")
@@ -88,13 +78,27 @@ def tile_picked_skippathbpolar_none_p_kernel(
         warm = sb.tile([P, 1], F32, name="warm")
         nc.scalar.activation(warm[:], quarter[:], ACT.Sqrt)
 
+        windows = {}
+        for name, engine in (("y", nc.vector), ("h", nc.gpsimd)):
+            for t in range(PACK):
+                windows[name, t] = sb.tile([P, 2 * S], F32, name="%s%d" % (name, t))
+                engine.memset(windows[name, t][:, S:], 0.0)
+
         xw = sb.tile([P, S], U32, name="xw", align_bytes=64)
         nc.vector.tensor_copy(xw[:], xw_all[:].indirect(offs_t[:]))
         xs = sb.tile([P, S], U8, name="xs", align_bytes=64)
         nc.vector.tensor_copy(xs[:], xs_all[:].indirect(offs_t[:]))
-        w1_codes, w1_scales = quantize_weight(
-            w1_raw, "w1", [(0, 256, "scalar"), (256, 512, "vector")], [(0, P), (P, H)]
-        )
+        w1_codes, w1_scales = operand("w1")
+        w1_pairs = w1_raw[:].rearrange("p j (m u e) -> p u m j e", u=2, e=2)
+        for u, split in enumerate((84, 0)):
+            grouped = sb.tile([P, 2, P, PACK], BF16, name="w1_bf%d" % u, align_bytes=64)
+            walk = grouped[:].rearrange("p e m j -> p m j e")
+            if split:
+                group(walk[:, :split], w1_pairs[:, u, :split], "vector")
+            group(walk[:, split:], w1_pairs[:, u, split:], "scalar")
+            for e in range(2):
+                t = 2 * u + e
+                quantize(w1_codes, w1_scales, slice(P * t, P * (t + 1)), grouped[:, e].rearrange("p m j -> p (m j)"))
 
         def product(codes, scales, rhs, rhs_scales, t, name, width):
             acc = ps.tile([P, S], F32, name="%s_ps%d" % (name, t))
@@ -109,18 +113,25 @@ def tile_picked_skippathbpolar_none_p_kernel(
                     start=True,
                     stop=True,
                 )
-            res = sb.tile([P, S], F32, name="%s%d" % (name, t))
-            nc.scalar.copy(res[:], acc[:])
+            res = windows[name, t]
+            nc.scalar.copy(res[:, :S], acc[:])
             return res
 
-        w2_codes, w2_scales = quantize_weight(w2_raw, "w2", [(0, 256, "scalar"), (256, 512, "vector")], [(0, H)])
+        w2_codes, w2_scales = operand("w2")
+        w2_bf = sb.tile([P, PACK, P, PACK], BF16, name="w2_bf", align_bytes=64)
+        for half, raw in enumerate(w2_raw):
+            nc.vector.tensor_copy(
+                out=w2_bf[:, :, 64 * half : 64 * (half + 1), :].rearrange("p (u e) m j -> p u m j e", e=2),
+                in_=raw[:].rearrange("p j (m u e) -> p u m j e", u=2, e=2),
+            )
+        quantize(w2_codes, w2_scales, slice(0, H), w2_bf[:].rearrange("p t m j -> p (t m j)"))
 
         def halves_of(lst):
             return [(slice(HALF * u, HALF * (u + 1)), lst[:, LIST_HALF * u : LIST_HALF * (u + 1)]) for u in range(2)]
 
-        def fetch(window, lst, name):
+        def fetch(window, lst, name, pieces):
             res = sb.tile([P, S], F32, name=name)
-            for cols, part in halves_of(lst):
+            for cols, part in halves_of(lst) if len(pieces) == 2 else [(pieces[0], lst[:])]:
                 nc.scalar.activation(res[:, cols], window[:].indirect(part), ACT.Copy)
             return res
 
@@ -155,18 +166,16 @@ def tile_picked_skippathbpolar_none_p_kernel(
 
         y5, y6 = {}, {}
         skips = [
-            (dst, slot, t, cols, part)
+            (dst, slot, t, lst)
             for t in range(PACK)
             for dst, lst, slot in ((y5, n5_t, "sq"), (y6, n6_t, "pair"))
-            for cols, part in halves_of(lst)
             if (slot, t) != ("sq", PACK - 1)
         ]
 
         def fetch_skips(count):
-            for dst, slot, t, cols, part in skips[:count]:
-                if t not in dst:
-                    dst[t] = sb.tile([P, S], F32, name="skip_%s%d" % (slot, t), tag="%s%d" % (slot, t))
-                nc.scalar.activation(dst[t][:, cols], y[t][:].indirect(part), ACT.Copy)
+            for dst, slot, t, lst in skips[:count]:
+                dst[t] = sb.tile([P, S], F32, name="skip_%s%d" % (slot, t), tag="%s%d" % (slot, t))
+                nc.scalar.activation(dst[t][:], y[t][:].indirect(lst[:]), ACT.Copy)
             return skips[count:]
 
         y.append(product(w1_codes, w1_scales, xw, xs, 0, "y", S))
@@ -174,24 +183,21 @@ def tile_picked_skippathbpolar_none_p_kernel(
         pair_up(1)
         root(0)
         pair_up(2)
-        skips = fetch_skips(2)
+        skips = fetch_skips(1)
         root(1)
         pair_up(3)
         skips = fetch_skips(1)
         root(2)
-        skips = fetch_skips(1)
         scale_plane(1)
-        skips = fetch_skips(1)
         root(3)
-        skips = fetch_skips(3)
+        skips = fetch_skips(2)
         scale_plane(2)
-        skips = fetch_skips(6)
+        skips = fetch_skips(3)
 
         z_bf = sb.tile([P, S, PACK], BF16, name="z_bf", tag="z_slot", align_bytes=64)
         z_codes = sb.tile([P, S], U32, name="z_codes", align_bytes=64)
         z_scales = sb.tile([P, S], U8, name="z_scales", align_bytes=64)
         last = PACK - 1
-        spans = [slice(0, HALF), slice(HALF, S)]
         for cols in spans:
             nc.vector.tensor_scalar(planes[:, last, cols], dt[last][:, cols], gain[:, last : last + 1], None, ALU.mult)
         for cols in spans:
@@ -206,8 +212,7 @@ def tile_picked_skippathbpolar_none_p_kernel(
                 in_=z_bf[:, cols, :].rearrange("p c t -> p (c t)"),
             )
         y5_last = sb.tile([P, S], F32, name="y5_last", tag="z_slot", align_bytes=64)
-        for cols, part in halves_of(n5_t):
-            nc.vector.tensor_copy(y5_last[:, cols], y[last][:].indirect(part))
+        nc.vector.tensor_copy(y5_last[:], y[last][:].indirect(n5_t[:]))
         y5[last] = y5_last
 
         out_rows = out.rearrange("(p t) c -> p t c", t=PACK)
@@ -217,15 +222,14 @@ def tile_picked_skippathbpolar_none_p_kernel(
             h[t] = product(w2_codes, w2_scales, z_codes, z_scales, t, "h", HALF if t == 0 else S)
             first[t] = sb.tile([P, S], F32, name="first%d" % t)
             if fused:
-                for cols, part in halves_of(n3_t):
-                    nc.vector.tensor_tensor(first[t][:, cols], h[t][:].indirect(part), y5[t][:, cols], ALU.add)
+                nc.vector.tensor_tensor(first[t][:], h[t][:].indirect(n3_t[:]), y5[t][:], ALU.add)
 
         def unfused(t):
-            h3 = fetch(h[t], n3_t, "h3_%d" % t)
+            h3 = fetch(h[t], n3_t, "h3_%d" % t, whole)
             nc.vector.tensor_tensor(first[t][:], h3[:], y5[t][:], ALU.add)
 
         def end(t, pieces):
-            h4 = fetch(h[t], n4_t, "h4_%d" % t)
+            h4 = fetch(h[t], n4_t, "h4_%d" % t, pieces)
             second = sb.tile([P, S], F32, name="second%d" % t)
             res = sb.tile([P, S], F32, name="res%d" % t)
             for cols in pieces:

@@ -135,7 +135,6 @@ def tile_picked_skippathbpolar_none_p_kernel(
                 nc.scalar.activation(res[:, cols], window[:].indirect(part), ACT.Copy)
             return res
 
-        planes = sb.tile([P, PACK, S], BF16, name="planes")
         y, ssum, dt = [], [], []
 
         def pair_up(t):
@@ -147,14 +146,19 @@ def tile_picked_skippathbpolar_none_p_kernel(
                 nc.scalar.activation(pair[:, 1, :], y[t][:].indirect(n2_t[:]), ACT.Copy)
             if t + 1 < PACK:
                 y.append(product(w1_codes, w1_scales, xw, xs, t + 1, "y", S))
-            else:
-                scale_plane(0)
             sq = sb.tile([P, 2, W], F32, name="sq%d" % t, tag="sq%d" % t)
-            nc.scalar.activation(sq[:], pair[:], ACT.Square)
+            nc.scalar.activation(sq[:, 0, :], pair[:, 0, :], ACT.Square, scale=2.0)
+            nc.scalar.activation(sq[:, 1, :], pair[:, 1, :], ACT.Square)
             dt.append(sb.tile([P, S], F32, name="dt%d" % t))
-            nc.vector.tensor_tensor(dt[t][:].indirect(n2_t[:]), pair[:, 1, :], pair[:, 0, :], ALU.add)
+            if t < 2:
+                nc.vector.tensor_tensor(dt[t][:].indirect(n2_t[:]), pair[:, 1, :], pair[:, 0, :], ALU.add)
+            else:
+                rb = sb.tile([P, W], F32, name="rb%d" % t)
+                nc.gpsimd.tensor_tensor(rb[:], pair[:, 1, :], pair[:, 0, :], ALU.add)
+                nc.vector.tensor_copy(dt[t][:].indirect(n2_t[:]), rb[:])
             ssum.append(sb.tile([P, W], F32, name="ssum%d" % t))
-            nc.vector.scalar_tensor_tensor(ssum[t][:], sq[:, 0, :], 4.0, sq[:, 1, :], ALU.mult, ALU.add)
+            adder = nc.vector if t == 0 else nc.gpsimd
+            adder.tensor_tensor(ssum[t][:], sq[:, 0, :], sq[:, 1, :], ALU.add)
 
         def root(t):
             ra = sb.tile([P, W], F32, name="ra%d" % t)
@@ -162,7 +166,7 @@ def tile_picked_skippathbpolar_none_p_kernel(
             nc.vector.tensor_copy(dt[t][:].indirect(n1_t[:]), ra[:])
 
         def scale_plane(t):
-            nc.scalar.activation(planes[:, t, :], dt[t][:], ACT.Copy, scale=gain[:, t : t + 1])
+            nc.gpsimd.tensor_scalar(planes[:, t, :], dt[t][:], gain[:, t : t + 1], 0.0, ALU.mult, ALU.add)
 
         y5, y6 = {}, {}
         skips = [
@@ -183,16 +187,17 @@ def tile_picked_skippathbpolar_none_p_kernel(
         pair_up(1)
         root(0)
         pair_up(2)
-        skips = fetch_skips(1)
         root(1)
         pair_up(3)
+        planes = sb.tile([P, PACK, S], BF16, name="planes", tag="sq3")
+        scale_plane(0)
         skips = fetch_skips(1)
         root(2)
         scale_plane(1)
+        skips = fetch_skips(1)
         root(3)
-        skips = fetch_skips(2)
         scale_plane(2)
-        skips = fetch_skips(3)
+        skips = fetch_skips(5)
 
         z_bf = sb.tile([P, S, PACK], BF16, name="z_bf", tag="z_slot", align_bytes=64)
         z_codes = sb.tile([P, S], U32, name="z_codes", align_bytes=64)

from contextlib import ExitStack

import concourse.mybir as mybir

K, T, S, H, W = 512, 2048, 512, 512, 256
FLOPS = 2 * K * H * S + 2 * H * H * S

F32 = mybir.dt.float32
BF16 = mybir.dt.bfloat16
I32 = mybir.dt.int32
U32 = mybir.dt.uint32
U16 = mybir.dt.uint16
U8 = mybir.dt.uint8
FP8X4 = mybir.dt.float8_e4m3fn_x4
ACT = mybir.ActivationFunctionType
ALU = mybir.AluOpType

P = 128
PACK = 4
HALF = 256
LIST_HALF = HALF // 16


def tile_picked_skippathbpolar_none_p_kernel(
    tc, x_words, x_scales, w1, gn, w2, offs, n1, n2, n3, n4, n5, n6, out
):
    nc = tc.nc
    with ExitStack() as ctx:
        sb = ctx.enter_context(tc.tile_pool(name="sb", bufs=1))
        ps = ctx.enter_context(tc.psum_pool(name="ps", bufs=1))

        def load_list(src, name):
            tl = sb.tile(list(src.shape), U16, name=name)
            nc.sync.dma_start(tl[:], src)
            return tl

        def group(dst, src, engine):
            if engine == "scalar":
                nc.scalar.activation(dst, src, ACT.Copy)
            else:
                nc.vector.tensor_copy(out=dst, in_=src)

        def operand(name):
            codes = sb.tile([P, H], U32, name=name + "_codes", align_bytes=64)
            scales = sb.tile([P, H], U8, name=name + "_scales", align_bytes=64)
            return codes, scales

        def quantize(codes, scales, cols, values):
            nc.vector.quantize_mx(out=codes[:, cols].bitcast(FP8X4), scales=scales[:, cols], in_=values)

        spans = [slice(0, HALF), slice(HALF, S)]
        xs_all = sb.tile([P, T], U8, name="xs_all")
        nc.vector.memset(xs_all[:].bitcast(I32), 0)
        for r in range(4):
            nc.sync.dma_start(xs_all[r:P:32, :].bitcast(I32), x_scales[0, r:16:4, :].bitcast(I32))
        offs_t = load_list(offs, "offs_t")
        xw_all = sb.tile([P, T], U32, name="xw_all")
        nc.sync.dma_start(xw_all[:].bitcast(I32), x_words[0].rearrange("p n t -> p (n t)").bitcast(I32))
        n1_t = load_list(n1, "n1_t")
        n2_t = load_list(n2, "n2_t")
        w1_raw = sb.tile([P, PACK, H], F32, name="w1_raw")
        nc.sync.dma_start(w1_raw[:], w1.rearrange("(p j) c -> p j c", j=PACK))
        w2_raw = []
        for cols in spans:
            raw = sb.tile([P, PACK, HALF], F32, name="w2_raw%d" % cols.start)
            nc.sync.dma_start(raw[:], w2.rearrange("(p j) c -> p j c", j=PACK)[:, :, cols])
            w2_raw.append(raw)
        gain = sb.tile([P, PACK], F32, name="gain")
        nc.sync.dma_start(gain[:], gn.rearrange("(p t) o -> p (t o)", t=PACK))
        n5_t = load_list(n5, "n5_t")
        n6_t = load_list(n6, "n6_t")
        n3_t = load_list(n3, "n3_t")
        n4_t = load_list(n4, "n4_t")

        quarter = sb.tile([P, 1], F32, name="quarter")
        nc.vector.memset(quarter[:], 0.25)

        warm = sb.tile([P, 1], F32, name="warm")
        nc.scalar.activation(warm[:], quarter[:], ACT.Sqrt)

        windows = {}
        for name, engine in (("y", nc.vector), ("h", nc.gpsimd)):
            for t in range(PACK):
                windows[name, t] = sb.tile([P, 2 * S], F32, name="%s%d" % (name, t))
                engine.memset(windows[name, t][:, S:], 0.0)

        xw = sb.tile([P, S], U32, name="xw", align_bytes=64)
        nc.vector.tensor_copy(xw[:], xw_all[:].indirect(offs_t[:]))
        xs = sb.tile([P, S], U8, name="xs", align_bytes=64)
        nc.vector.tensor_copy(xs[:], xs_all[:].indirect(offs_t[:]))
        w1_codes, w1_scales = operand("w1")
        w1_pairs = w1_raw[:].rearrange("p j (m u e) -> p u m j e", u=2, e=2)
        for u, split in enumerate((84, 0)):
            grouped = sb.tile([P, 2, P, PACK], BF16, name="w1_bf%d" % u, align_bytes=64)
            walk = grouped[:].rearrange("p e m j -> p m j e")
            if split:
                group(walk[:, :split], w1_pairs[:, u, :split], "vector")
            group(walk[:, split:], w1_pairs[:, u, split:], "scalar")
            for e in range(2):
                t = 2 * u + e
                quantize(w1_codes, w1_scales, slice(P * t, P * (t + 1)), grouped[:, e].rearrange("p m j -> p (m j)"))

        def product(codes, scales, rhs, rhs_scales, t, name, width):
            acc = ps.tile([P, S], F32, name="%s_ps%d" % (name, t))
            cols = slice(P * t, P * (t + 1))
            for c in range(0, S, width):
                nc.tensor.matmul_mx(
                    out=acc[:, c : c + width],
                    lhsT=codes[:, cols].bitcast(FP8X4),
                    lhsT_scale=scales[:, cols],
                    rhs=rhs[:, c : c + width].bitcast(FP8X4),
                    rhs_scale=rhs_scales[:, c : c + width],
                    start=True,
                    stop=True,
                )
            res = windows[name, t]
            nc.scalar.copy(res[:, :S], acc[:])
            return res

        w2_codes, w2_scales = operand("w2")
        w2_bf = sb.tile([P, PACK, P, PACK], BF16, name="w2_bf", align_bytes=64)
        for half, raw in enumerate(w2_raw):
            nc.vector.tensor_copy(
                out=w2_bf[:, :, 64 * half : 64 * (half + 1), :].rearrange("p (u e) m j -> p u m j e", e=2),
                in_=raw[:].rearrange("p j (m u e) -> p u m j e", u=2, e=2),
            )
        quantize(w2_codes, w2_scales, slice(0, H), w2_bf[:].rearrange("p t m j -> p (t m j)"))

        def halves_of(lst):
            return [(slice(HALF * u, HALF * (u + 1)), lst[:, LIST_HALF * u : LIST_HALF * (u + 1)]) for u in range(2)]

        def fetch(window, lst, name, pieces):
            res = sb.tile([P, S], F32, name=name)
            for cols, part in halves_of(lst) if len(pieces) == 2 else [(pieces[0], lst[:])]:
                nc.scalar.activation(res[:, cols], window[:].indirect(part), ACT.Copy)
            return res

        y, ssum, dt = [], [], []

        def pair_up(t):
            pair = sb.tile([P, 2, W], F32, name="pair%d" % t, tag="pair%d" % t)
            nc.scalar.activation(pair[:, 0, :], y[t][:].indirect(n1_t[:]), ACT.Copy, scale=-0.5)
            if t == 0:
                nc.vector.tensor_copy(pair[:, 1, :], y[t][:].indirect(n2_t[:]))
            else:
                nc.scalar.activation(pair[:, 1, :], y[t][:].indirect(n2_t[:]), ACT.Copy)
            if t + 1 < PACK:
                y.append(product(w1_codes, w1_scales, xw, xs, t + 1, "y", S))
            sq = sb.tile([P, 2, W], F32, name="sq%d" % t, tag="sq%d" % t)
            nc.scalar.activation(sq[:, 0, :], pair[:, 0, :], ACT.Square, scale=2.0)
            nc.scalar.activation(sq[:, 1, :], pair[:, 1, :], ACT.Square)
            dt.append(sb.tile([P, S], F32, name="dt%d" % t))
            if t < 2:
                nc.vector.tensor_tensor(dt[t][:].indirect(n2_t[:]), pair[:, 1, :], pair[:, 0, :], ALU.add)
            else:
                rb = sb.tile([P, W], F32, name="rb%d" % t)
                nc.gpsimd.tensor_tensor(rb[:], pair[:, 1, :], pair[:, 0, :], ALU.add)
                nc.vector.tensor_copy(dt[t][:].indirect(n2_t[:]), rb[:])
            ssum.append(sb.tile([P, W], F32, name="ssum%d" % t))
            adder = nc.vector if t == 0 else nc.gpsimd
            adder.tensor_tensor(ssum[t][:], sq[:, 0, :], sq[:, 1, :], ALU.add)

        def root(t):
            ra = sb.tile([P, W], F32, name="ra%d" % t)
            nc.scalar.activation(ra[:], ssum[t][:], ACT.Sqrt, bias=quarter[:])
            nc.vector.tensor_copy(dt[t][:].indirect(n1_t[:]), ra[:])

        def scale_plane(t):
            nc.gpsimd.tensor_scalar(planes[:, t, :], dt[t][:], gain[:, t : t + 1], 0.0, ALU.mult, ALU.add)

        y5, y6 = {}, {}
        skips = [
            (dst, slot, t, lst)
            for t in range(PACK)
            for dst, lst, slot in ((y5, n5_t, "sq"), (y6, n6_t, "pair"))
            if (slot, t) != ("sq", PACK - 1)
        ]

        def fetch_skips(count):
            for dst, slot, t, lst in skips[:count]:
                dst[t] = sb.tile([P, S], F32, name="skip_%s%d" % (slot, t), tag="%s%d" % (slot, t))
                nc.scalar.activation(dst[t][:], y[t][:].indirect(lst[:]), ACT.Copy)
            return skips[count:]

        y.append(product(w1_codes, w1_scales, xw, xs, 0, "y", S))
        pair_up(0)
        pair_up(1)
        root(0)
        pair_up(2)
        root(1)
        pair_up(3)
        planes = sb.tile([P, PACK, S], BF16, name="planes", tag="sq3")
        scale_plane(0)
        skips = fetch_skips(1)
        root(2)
        scale_plane(1)
        skips = fetch_skips(1)
        root(3)
        scale_plane(2)
        skips = fetch_skips(5)

        z_bf = sb.tile([P, S, PACK], BF16, name="z_bf", tag="z_slot", align_bytes=64)
        z_codes = sb.tile([P, S], U32, name="z_codes", align_bytes=64)
        z_scales = sb.tile([P, S], U8, name="z_scales", align_bytes=64)
        last = PACK - 1
        for cols in spans:
            nc.vector.tensor_scalar(planes[:, last, cols], dt[last][:, cols], gain[:, last : last + 1], None, ALU.mult)
        for cols in spans:
            nc.vector.tensor_copy(
                z_bf[:, cols, :].rearrange("p (c i) t -> p c t i", i=4),
                planes[:, :, cols].rearrange("p t (c i) -> p c t i", i=4),
            )
        for cols in spans:
            nc.vector.quantize_mx(
                out=z_codes[:, cols].bitcast(FP8X4),
                scales=z_scales[:, cols],
                in_=z_bf[:, cols, :].rearrange("p c t -> p (c t)"),
            )
        y5_last = sb.tile([P, S], F32, name="y5_last", tag="z_slot", align_bytes=64)
        nc.vector.tensor_copy(y5_last[:], y[last][:].indirect(n5_t[:]))
        y5[last] = y5_last

        out_rows = out.rearrange("(p t) c -> p t c", t=PACK)
        h, first = {}, {}

        def start(t, fused):
            h[t] = product(w2_codes, w2_scales, z_codes, z_scales, t, "h", HALF if t == 0 else S)
            first[t] = sb.tile([P, S], F32, name="first%d" % t)
            if fused:
                nc.vector.tensor_tensor(first[t][:], h[t][:].indirect(n3_t[:]), y5[t][:], ALU.add)

        def unfused(t):
            h3 = fetch(h[t], n3_t, "h3_%d" % t, whole)
            nc.vector.tensor_tensor(first[t][:], h3[:], y5[t][:], ALU.add)

        def end(t, pieces):
            h4 = fetch(h[t], n4_t, "h4_%d" % t, pieces)
            second = sb.tile([P, S], F32, name="second%d" % t)
            res = sb.tile([P, S], F32, name="res%d" % t)
            for cols in pieces:
                nc.vector.tensor_tensor(second[:, cols], h4[:, cols], y6[t][:, cols], ALU.add)
                nc.vector.tensor_tensor(res[:, cols], first[t][:, cols], second[:, cols], ALU.max)
                nc.sync.dma_start(out_rows[:, t, cols], res[:, cols])

        whole = [slice(0, S)]
        start(0, True)
        start(1, True)
        end(0, whole)
        start(2, True)
        end(1, whole)
        start(3, False)
        end(2, whole)
        unfused(3)
        end(3, spans)
